import numpy as np
import ml_dtypes


def mxq(x, axis, fmt="e4m3"):
    dtype, down = {"e4m3": (ml_dtypes.float8_e4m3fn, 7), "e5m2": (ml_dtypes.float8_e5m2, 14)}[fmt]
    v = np.moveaxis(np.asarray(x, np.float32).astype(ml_dtypes.bfloat16).astype(np.float64), axis, -1)
    blocks = v.reshape(v.shape[:-1] + (-1, 32))
    amax = np.abs(blocks).max(-1, keepdims=True)
    byte = np.maximum(np.where(amax > 0, np.frexp(amax)[1] - 1 + 127, 0) - down, 1)
    scale = np.exp2(byte - 127.0)
    codes = (blocks / scale).astype(np.float32).astype(dtype).astype(np.float64)
    return np.moveaxis((codes * scale).reshape(v.shape), -1, axis)


WIDE = False


def mx_kscale(k):
    if not WIDE:
        return np.ones(k)
    levels = np.array([30, -30])
    if k % 512:
        return np.exp2(np.random.permutation(np.resize(levels, k // 32))).repeat(32)
    a = np.empty((k // 512, 16))
    for p in range(k // 512):
        a[p, :8] = np.random.permutation(np.resize(levels, 8))
        for g in range(8):
            far = levels[np.abs(levels - a[p, g]) >= 10]
            a[p, g + 8] = far[np.random.randint(len(far))]
    return np.exp2(a.ravel()).repeat(32)


def f64(x):
    return np.asarray(x).astype(np.float64)


def striped(idx):
    return np.tile(np.asarray(idx).reshape(-1, 16).T, (8, 1)).astype(np.uint16)


def unstriped(offs):
    return offs[:16].T.reshape(-1).astype(np.int64)


def striped8(idx):
    return np.asarray(idx).reshape(8, -1, 16).transpose(0, 2, 1).reshape(128, -1).astype(np.uint16)


def unstriped8(offs):
    return offs.reshape(8, 16, -1).transpose(0, 2, 1).reshape(8, -1).astype(np.int64)


def pick8(x, idx, run):
    r = np.arange(len(x))
    return x[r[:, None], idx[r % (8 * run) // run]]


E2M1 = np.array([0.0, 0.5, 1.0, 1.5, 2.0, 3.0, 4.0, 6.0, -0.0, -0.5, -1.0, -1.5, -2.0, -3.0, -4.0, -6.0])


def pack_weight(w, fmt):
    k, n = w.shape
    w = f64(np.asarray(w, np.float32).astype(ml_dtypes.bfloat16)).reshape(k // 32, 32, n)
    amax = np.abs(w).max(1)
    if fmt in ("e4m3", "e5m2"):
        byte = np.frexp(amax)[1] - 1 + 127 - (7 if fmt == "e4m3" else 14)
    else:
        mant, ex = np.frexp(amax / 6.0)
        byte = np.where(mant > 0.5, ex, ex - 1) + 127
    byte = np.clip(np.where(amax > 0, byte, 1), 1, 254)
    scaled = (w * np.exp2(127.0 - byte)[:, None, :]).reshape(k, n).astype(np.float32)
    by_word = np.ascontiguousarray(scaled.reshape(k // 512, 128, 4, n).transpose(0, 1, 3, 2))
    if fmt in ("e4m3", "e5m2"):
        words = by_word.astype(ml_dtypes.float8_e4m3fn if fmt == "e4m3" else ml_dtypes.float8_e5m2).view(np.uint8)
    else:
        c = by_word.astype(ml_dtypes.float4_e2m1fn).view(np.uint8) & 0xF
        words = (c[..., 0::2] | (c[..., 1::2] << 4)).reshape(k // 512, 128, 2 * n)
    return np.ascontiguousarray(words), np.ascontiguousarray(byte.astype(np.uint8).reshape(k // 512, 16, n))


def unpack_weight(words, scales, fmt):
    g, _, n = scales.shape
    words = np.ascontiguousarray(words).reshape(g, 128, n, -1)
    if fmt in ("e4m3", "e5m2"):
        vals = words.view(ml_dtypes.float8_e4m3fn if fmt == "e4m3" else ml_dtypes.float8_e5m2).astype(np.float64)
    else:
        nib = np.empty((g, 128, n, 4), np.uint8)
        nib[..., 0::2] = words & 0xF
        nib[..., 1::2] = words >> 4
        vals = E2M1[nib]
    vals = vals * np.repeat(np.exp2(scales.astype(np.float64) - 127.0), 8, axis=1)[..., None]
    return vals.transpose(0, 1, 3, 2).reshape(g * 512, n)


K, T, J, R, F, Z, C, O, N, E = 512, 1024, 256, 512, 512, 1024, 512, 128, 256, 512


def setup_inputs():
    n = np.random.standard_normal
    idx = np.random.permutation(T)[:J]
    idx2 = np.random.permutation(Z)[:J]
    idx3 = np.stack([np.random.permutation(C)[:J] for _ in range(8)])
    idx4 = np.random.permutation(C)[:O]
    idx5 = np.random.permutation(C)[:O]
    idx6 = np.random.permutation(J)[:O]
    idx7 = np.stack([np.random.permutation(E)[:O] for _ in range(8)])
    fk = mx_kscale(K)
    ff = mx_kscale(F)
    fr = mx_kscale(R)
    xtp = pack_weight(n((K, T)) / fk[:, None], "e2m1")
    xop = pack_weight(n((F, Z)) / ff[:, None], "e4m3")
    wp = pack_weight(n((K, R)) * 1 / np.sqrt(K) * fk[:, None] * fr, "e4m3")
    w0p = pack_weight(n((F, R)) * 1 / np.sqrt(F) * ff[:, None] * fr, "e2m1")
    w2p = pack_weight(n((F, R)) * 1 / np.sqrt(F) * ff[:, None] * fr, "e5m2")
    wbp = pack_weight(n((R, N)) * 1 / np.sqrt(R) / fr[:, None], "e2m1")
    return {
        "xt_words": xtp[0],
        "xt_scales": xtp[1],
        "xo_words": xop[0],
        "xo_scales": xop[1],
        "w_words": wp[0],
        "w_scales": wp[1],
        "w0_words": w0p[0],
        "w0_scales": w0p[1],
        "w2_words": w2p[0],
        "w2_scales": w2p[1],
        "sa": (np.random.uniform(0.5, 1.6, (R, 1))).astype(np.float32),
        "sb": (np.random.uniform(0.5, 1.6, (R, 1))).astype(np.float32),
        "sd": (np.random.uniform(0.5, 1.6, (R, 1))).astype(np.float32),
        "wb_words": wbp[0],
        "wb_scales": wbp[1],
        "offs": striped(idx),
        "offs2": striped(idx2),
        "offs3": striped8(idx3),
        "offs4": striped(idx4),
        "offs5": striped(idx5),
        "offs6": striped(idx6),
        "offs7": striped8(idx7),
    }


def reference(xt_words, xt_scales, xo_words, xo_scales, w_words, w_scales, w0_words, w0_scales, w2_words, w2_scales, sa, sb, sd, wb_words, wb_scales, offs, offs2, offs3, offs4, offs5, offs6, offs7):
    idx = unstriped(offs)
    idx2 = unstriped(offs2)
    idx3 = unstriped8(offs3)
    idx4 = unstriped(offs4)
    idx5 = unstriped(offs5)
    idx6 = unstriped(offs6)
    idx7 = unstriped8(offs7)
    xtu = unpack_weight(xt_words, xt_scales, "e2m1")
    xou = unpack_weight(xo_words, xo_scales, "e4m3")
    wu = unpack_weight(w_words, w_scales, "e4m3")
    w0u = unpack_weight(w0_words, w0_scales, "e2m1")
    w2u = unpack_weight(w2_words, w2_scales, "e5m2")
    wbu = unpack_weight(wb_words, wb_scales, "e2m1")
    xtidxg = xtu[:, idx]
    xoidx2g = xou[:, idx2]
    a = wu.T @ xtidxg + w0u.T @ xoidx2g
    b = w2u.T @ xoidx2g
    pw = np.zeros((R, C))
    pw[np.arange(R)[:, None], idx3[np.arange(R) % 512 // 64]] = a
    hid = np.maximum(pw[:, idx4] * f64(sa), pw[:, idx5] * f64(sb)) - b[:, idx6] * f64(sd)
    hidq = mxq(hid, 0, "e5m2")
    p = wbu.T @ hidq
    y = np.zeros((N, E))
    y[np.arange(N)[:, None], idx7[np.arange(N) % 128 // 16]] = p
    return y

@@ -1,0 +1,216 @@
+from contextlib import ExitStack
+
+import concourse.mybir as mybir
+
+T, J, R, Z, C, O, N, E = 1024, 256, 512, 1024, 512, 128, 256, 512
+FLOPS = 436207616
+
+F32 = mybir.dt.float32
+BF16 = mybir.dt.bfloat16
+I32 = mybir.dt.int32
+U32 = mybir.dt.uint32
+U16 = mybir.dt.uint16
+U8 = mybir.dt.uint8
+E4M3 = mybir.dt.float8_e4m3fn_x4
+E5M2 = mybir.dt.float8_e5m2_x4
+E2M1 = mybir.dt.float4_e2m1fn_x4
+COPY = mybir.ActivationFunctionType.Copy
+ALU = mybir.AluOpType
+
+P = 128
+PACK = 4
+LINE = 16
+
+
+def tile_list_ownthree_noted_one_ownpage_kernel(
+    tc, xt_words, xt_scales, xo_words, xo_scales, w_words, w_scales, w0_words, w0_scales, w2_words, w2_scales,
+    sa, sb, sd, wb_words, wb_scales, offs, offs2, offs3, offs4, offs5, offs6, offs7, out,
+):
+    nc = tc.nc
+    with ExitStack() as ctx:
+        held = ctx.enter_context(tc.tile_pool(name="held", bufs=1))
+        psum = ctx.enter_context(tc.psum_pool(name="psum", bufs=1))
+
+        def tile(name, cols, dtype):
+            return held.tile([P, cols], dtype, name=name, align_bytes=64)
+
+        def load_list(name, src):
+            lst = held.tile(list(src.shape), U16, name=name)
+            nc.sync.dma_start(lst[:], src)
+            return lst
+
+        def load_words(queue, name, src, cols, dtype):
+            words = tile(name, cols, dtype)
+            queue.dma_start(words[:].bitcast(I32), src.bitcast(I32))
+            return words
+
+        def zeroed(name, cols):
+            plane = tile(name, cols, U8)
+            nc.vector.memset(plane[:].bitcast(I32), 0)
+            return plane
+
+        def load_plane(queue, plane, src):
+            for q in range(4):
+                queue.dma_start(plane[32 * q : 32 * q + 4, :].bitcast(I32), src[0, 4 * q : 4 * q + 4, :].bitcast(I32))
+
+        def load_halves(queue, plane, src):
+            rows = src[0].bitcast(I32).rearrange("(a b r) n -> b r a n", a=2, b=2)
+            for b in range(2):
+                queue.dma_start(plane[32 * b : 32 * b + 4, :].bitcast(I32).rearrange("r (a n) -> r a n", a=2), rows[b])
+
+        def spread(plane, cols):
+            nc.vector.tensor_copy(plane[64:128, 0:cols].bitcast(I32), plane[0:64, cols : 2 * cols].bitcast(I32))
+
+        def deal_first(name, src, dtype):
+            first = tile(name, P, dtype)
+            nc.vector.tensor_copy(first[:], src[:, 0:R:PACK])
+            return first
+
+        def deal_rest(name, src, dtype, run):
+            rest = tile(name, (PACK - 1) * P, dtype)
+            nc.vector.tensor_copy(
+                rest[:].rearrange("p (t c i) -> p c t i", t=PACK - 1, i=run),
+                src[:, 0:R].rearrange("p (c i t) -> p c t i", i=run, t=PACK)[:, :, 1:PACK, :],
+            )
+            return rest
+
+        def deal_all(name, src, dtype, run):
+            dealt = tile(name, R, dtype)
+            nc.vector.tensor_copy(
+                dealt[:].rearrange("p (t c i) -> p c t i", t=PACK, i=run),
+                src[:, 0:R].rearrange("p (c i t) -> p c t i", i=run, t=PACK),
+            )
+            return dealt
+
+        flat = lambda words: words[0].rearrange("p n t -> p (n t)")
+
+        xt_s = zeroed("xt_s", T)
+        xo_s = zeroed("xo_s", Z)
+        w0_s = zeroed("w0_s", 2 * R)
+        w_s = zeroed("w_s", 2 * R)
+        w2_s = zeroed("w2_s", 2 * R)
+        wb_s = zeroed("wb_s", 2 * N)
+
+        xt_w = load_words(nc.sync, "xt_w", xt_words[0], T, U16)
+        l1 = load_list("l1", offs)
+        l2 = load_list("l2", offs2)
+        load_plane(nc.sync, xt_s, xt_scales)
+        xo_w = load_words(nc.sync, "xo_w", flat(xo_words), Z, U32)
+        load_plane(nc.sync, xo_s, xo_scales)
+        w0_w = load_words(nc.sync, "w0_w", w0_words[0], R, U16)
+        w_w = load_words(nc.sync, "w_w", flat(w_words), R, U32)
+        load_halves(nc.sync, w0_s, w0_scales)
+        load_halves(nc.sync, w_s, w_scales)
+        l3 = load_list("l3", offs3)
+        w2_w = load_words(nc.sync, "w2_w", flat(w2_words), R, U32)
+        l4 = load_list("l4", offs4)
+        l5 = load_list("l5", offs5)
+        l6 = load_list("l6", offs6)
+        l7 = load_list("l7", offs7)
+
+        load_halves(nc.gpsimd, w2_s, w2_scales)
+        factors = []
+        for name, src in (("sa_t", sa), ("sb_t", sb), ("sd_t", sd)):
+            fac = held.tile([P, PACK], F32, name=name)
+            nc.gpsimd.dma_start(fac[:], src.rearrange("(p t) o -> p (t o)", t=PACK))
+            factors.append(fac)
+        sa_t, sb_t, sd_t = factors
+        wb_w = load_words(nc.gpsimd, "wb_w", wb_words[0], N, U16)
+        load_halves(nc.gpsimd, wb_s, wb_scales)
+
+        boards = []
+        for t in range(PACK):
+            board = tile("board%d" % t, C, F32)
+            nc.vector.memset(board[:], 0.0)
+            boards.append(board)
+
+        xt_g = tile("xt_g", J, U16)
+        xt_gs = tile("xt_gs", J, U8)
+        xo_g = tile("xo_g", J, U32)
+        xo_gs = tile("xo_gs", J, U8)
+        nc.vector.tensor_copy(xt_g[:], xt_w[:].indirect(l1[:]))
+        nc.vector.tensor_copy(xt_gs[:], xt_s[:].indirect(l1[:]))
+        nc.vector.tensor_copy(xo_g[:], xo_w[:].indirect(l2[:]))
+        nc.vector.tensor_copy(xo_gs[:], xo_s[:].indirect(l2[:]))
+
+        w0_w0 = deal_first("w0_w0", w0_w, U16)
+        w_w0 = deal_first("w_w0", w_w, U32)
+        spread(w0_s, R)
+        spread(w_s, R)
+        w0_s0 = deal_first("w0_s0", w0_s, U8)
+        w_s0 = deal_first("w_s0", w_s, U8)
+
+        def product_a(t, w0c, w0s, wc, ws):
+            acc = psum.tile([P, J], F32, name="acc_a", bufs=3)
+            nc.tensor.matmul_mx(out=acc[:], lhsT=w0c.bitcast(E2M1), lhsT_scale=w0s, rhs=xo_g[:].bitcast(E4M3),
+                                rhs_scale=xo_gs[:], start=True, stop=False)
+            nc.tensor.matmul_mx(out=acc[:], lhsT=wc.bitcast(E4M3), lhsT_scale=ws, rhs=xt_g[:].bitcast(E2M1),
+                                rhs_scale=xt_gs[:], start=False, stop=True)
+            a_t = tile("a%d" % t, J, F32)
+            if t == 0:
+                nc.scalar.copy(a_t[:], acc[:])
+            else:
+                nc.vector.tensor_copy(a_t[:], acc[:])
+            nc.scalar.activation(boards[t][:].indirect(l3[:]), a_t[:], COPY)
+
+        product_a(0, w0_w0[:], w0_s0[:], w_w0[:], w_s0[:])
+
+        w0_w1 = deal_rest("w0_w1", w0_w, U16, 8)
+        w_w1 = deal_rest("w_w1", w_w, U32, 4)
+        w0_s1 = deal_rest("w0_s1", w0_s, U8, 16)
+        w_s1 = deal_rest("w_s1", w_s, U8, 16)
+
+        hid = held.tile([P, O, PACK], BF16, name="hid", align_bytes=64)
+
+        def later_a(t):
+            cols = slice((t - 1) * P, t * P)
+            product_a(t, w0_w1[:, cols], w0_s1[:, cols], w_w1[:, cols], w_s1[:, cols])
+
+        later_a(1)
+
+        w2_wd = deal_all("w2_wd", w2_w, U32, 4)
+        spread(w2_s, R)
+        w2_sd = deal_all("w2_sd", w2_s, U8, 16)
+
+        def combine(t):
+            cols = slice(t * P, (t + 1) * P)
+            acc = psum.tile([P, J], F32, name="acc_b", bufs=3)
+            nc.tensor.matmul_mx(out=acc[:], lhsT=w2_wd[:, cols].bitcast(E5M2), lhsT_scale=w2_sd[:, cols],
+                                rhs=xo_g[:].bitcast(E4M3), rhs_scale=xo_gs[:], start=True, stop=True)
+            b_t = tile("b%d" % t, J, F32)
+            nc.vector.tensor_copy(b_t[:], acc[:])
+            left = tile("left%d" % t, O, F32)
+            right = tile("right%d" % t, O, F32)
+            third = tile("third%d" % t, O, F32)
+            nc.scalar.activation(left[:], boards[t][:].indirect(l4[:]), COPY, scale=sa_t[:, t : t + 1])
+            nc.scalar.activation(right[:], boards[t][:].indirect(l5[:]), COPY, scale=sb_t[:, t : t + 1])
+            nc.scalar.activation(third[:], b_t[:].indirect(l6[:]), COPY, scale=sd_t[:, t : t + 1])
+            larger = tile("larger%d" % t, O, F32)
+            nc.vector.tensor_tensor(larger[:], left[:], right[:], ALU.max)
+            nc.vector.tensor_tensor(hid[:, :, t], larger[:], third[:], ALU.subtract)
+
+        for t in range(PACK):
+            combine(t)
+            if t + 2 < PACK:
+                later_a(t + 2)
+
+        pages = []
+        for u in range(N // P):
+            page = tile("page%d" % u, E, F32)
+            nc.vector.memset(page[:], 0.0)
+            pages.append(page)
+        spread(wb_s, N)
+
+        hid_q = tile("hid_q", O, U32)
+        hid_s = tile("hid_s", O, U8)
+        nc.vector.quantize_mx(out=hid_q[:].bitcast(E5M2), scales=hid_s[:], in_=hid[:].rearrange("p o t -> p (o t)"))
+
+        for u in range(N // P):
+            cols = slice(u * P, (u + 1) * P)
+            acc = psum.tile([P, O], F32, name="acc_p", bufs=2)
+            nc.tensor.matmul_mx(out=acc[:], lhsT=wb_w[:, cols].bitcast(E2M1), lhsT_scale=wb_s[:, cols],
+                                rhs=hid_q[:].bitcast(E5M2), rhs_scale=hid_s[:], start=True, stop=True)
+            p_u = tile("p%d" % u, O, F32)
+            nc.vector.tensor_copy(p_u[:], acc[:])
+            nc.scalar.activation(pages[u][:].indirect(l7[:]), p_u[:], COPY)
+            nc.sync.dma_start(out[u * P : (u + 1) * P, :], pages[u][:])

@@ -31,8 +31,8 @@ def tile_list_ownthree_noted_one_ownpage_kernel(
         held = ctx.enter_context(tc.tile_pool(name="held", bufs=1))
         psum = ctx.enter_context(tc.psum_pool(name="psum", bufs=1))
 
-        def tile(name, cols, dtype):
-            return held.tile([P, cols], dtype, name=name, align_bytes=64)
+        def tile(name, cols, dtype, tag=""):
+            return held.tile([P, cols], dtype, name=name, tag=tag or name, align_bytes=64)
 
         def load_list(name, src):
             lst = held.tile(list(src.shape), U16, name=name)
@@ -43,6 +43,11 @@ def tile_list_ownthree_noted_one_ownpage_kernel(
             words = tile(name, cols, dtype)
             queue.dma_start(words[:].bitcast(I32), src.bitcast(I32))
             return words
+
+        def load_factor(name, src):
+            fac = held.tile([P, PACK], F32, name=name)
+            nc.sync.dma_start(fac[:], src.rearrange("(p t) o -> p (t o)", t=PACK))
+            return fac
 
         def zeroed(name, cols):
             plane = tile(name, cols, U8)
@@ -61,22 +66,9 @@ def tile_list_ownthree_noted_one_ownpage_kernel(
         def spread(plane, cols):
             nc.vector.tensor_copy(plane[64:128, 0:cols].bitcast(I32), plane[0:64, cols : 2 * cols].bitcast(I32))
 
-        def deal_first(name, src, dtype):
-            first = tile(name, P, dtype)
-            nc.vector.tensor_copy(first[:], src[:, 0:R:PACK])
-            return first
-
-        def deal_rest(name, src, dtype, run):
-            rest = tile(name, (PACK - 1) * P, dtype)
-            nc.vector.tensor_copy(
-                rest[:].rearrange("p (t c i) -> p c t i", t=PACK - 1, i=run),
-                src[:, 0:R].rearrange("p (c i t) -> p c t i", i=run, t=PACK)[:, :, 1:PACK, :],
-            )
-            return rest
-
-        def deal_all(name, src, dtype, run):
+        def deal_all(copy, name, src, dtype, run):
             dealt = tile(name, R, dtype)
-            nc.vector.tensor_copy(
+            copy(
                 dealt[:].rearrange("p (t c i) -> p c t i", t=PACK, i=run),
                 src[:, 0:R].rearrange("p (c i t) -> p c t i", i=run, t=PACK),
             )
@@ -84,39 +76,60 @@ def tile_list_ownthree_noted_one_ownpage_kernel(
 
         flat = lambda words: words[0].rearrange("p n t -> p (n t)")
 
-        xt_s = zeroed("xt_s", T)
-        xo_s = zeroed("xo_s", Z)
         w0_s = zeroed("w0_s", 2 * R)
         w_s = zeroed("w_s", 2 * R)
+        xt_h = zeroed("xt_h", 2 * T)
+        xo_h = zeroed("xo_h", 2 * Z)
         w2_s = zeroed("w2_s", 2 * R)
-        wb_s = zeroed("wb_s", 2 * N)
+        wb_s = zeroed("wb_s", N)
 
-        xt_w = load_words(nc.sync, "xt_w", xt_words[0], T, U16)
         l1 = load_list("l1", offs)
         l2 = load_list("l2", offs2)
-        load_plane(nc.sync, xt_s, xt_scales)
-        xo_w = load_words(nc.sync, "xo_w", flat(xo_words), Z, U32)
-        load_plane(nc.sync, xo_s, xo_scales)
-        w0_w = load_words(nc.sync, "w0_w", w0_words[0], R, U16)
-        w_w = load_words(nc.sync, "w_w", flat(w_words), R, U32)
+        xt_w = load_words(nc.sync, "xt_w", xt_words[0], T, U16)
         load_halves(nc.sync, w0_s, w0_scales)
         load_halves(nc.sync, w_s, w_scales)
+        xo_w = load_words(nc.sync, "xo_w", flat(xo_words), Z, U32)
+        load_halves(nc.sync, xt_h, xt_scales)
+        load_halves(nc.sync, xo_h, xo_scales)
+        w0_w = load_words(nc.sync, "w0_w", w0_words[0], R, U16)
+        w_w = load_words(nc.sync, "w_w", flat(w_words), R, U32)
         l3 = load_list("l3", offs3)
         w2_w = load_words(nc.sync, "w2_w", flat(w2_words), R, U32)
         l4 = load_list("l4", offs4)
+        sa_t = load_factor("sa_t", sa)
         l5 = load_list("l5", offs5)
+        sb_t = load_factor("sb_t", sb)
+        load_halves(nc.sync, w2_s, w2_scales)
         l6 = load_list("l6", offs6)
+        sd_t = load_factor("sd_t", sd)
+        wb_w = load_words(nc.sync, "wb_w", wb_words[0], N, U16)
+        load_plane(nc.sync, wb_s, wb_scales)
         l7 = load_list("l7", offs7)
 
-        load_halves(nc.gpsimd, w2_s, w2_scales)
-        factors = []
-        for name, src in (("sa_t", sa), ("sb_t", sb), ("sd_t", sd)):
-            fac = held.tile([P, PACK], F32, name=name)
-            nc.gpsimd.dma_start(fac[:], src.rearrange("(p t) o -> p (t o)", t=PACK))
-            factors.append(fac)
-        sa_t, sb_t, sd_t = factors
-        wb_w = load_words(nc.gpsimd, "wb_w", wb_words[0], N, U16)
-        load_halves(nc.gpsimd, wb_s, wb_scales)
+        xt_g = tile("xt_g", J, U16)
+        xt_gs = tile("xt_gs", J, U8)
+        xo_g = tile("xo_g", J, U32)
+        xo_gs = tile("xo_gs", J, U8)
+        nc.vector.tensor_copy(xt_g[:], xt_w[:].indirect(l1[:]))
+        spread(w0_s, R)
+        spread(w_s, R)
+        w0_sd = deal_all(nc.vector.tensor_copy, "w0_sd", w0_s, U8, 16)
+        w_sd = deal_all(nc.vector.tensor_copy, "w_sd", w_s, U8, 16)
+        nc.vector.tensor_copy(xo_g[:], xo_w[:].indirect(l2[:]))
+
+        xt_s = tile("xt_s", T, U8)
+        xo_s = tile("xo_s", Z, U8)
+        for half in range(2):
+            for plane, halves, cols in ((xt_s, xt_h, T), (xo_s, xo_h, Z)):
+                nc.vector.tensor_copy(
+                    plane[64 * half : 64 * half + 64, :].bitcast(I32),
+                    halves[0:64, half * cols : (half + 1) * cols].bitcast(I32),
+                )
+        nc.vector.tensor_copy(xt_gs[:], xt_s[:].indirect(l1[:]))
+        nc.vector.tensor_copy(xo_gs[:], xo_s[:].indirect(l2[:]))
+
+        w0_wd = deal_all(nc.scalar.copy, "w0_wd", w0_w, U16, 8)
+        w_wd = deal_all(nc.scalar.copy, "w_wd", w_w, U32, 4)
 
         boards = []
         for t in range(PACK):
@@ -124,28 +137,12 @@ def tile_list_ownthree_noted_one_ownpage_kernel(
             nc.vector.memset(board[:], 0.0)
             boards.append(board)
 
-        xt_g = tile("xt_g", J, U16)
-        xt_gs = tile("xt_gs", J, U8)
-        xo_g = tile("xo_g", J, U32)
-        xo_gs = tile("xo_gs", J, U8)
-        nc.vector.tensor_copy(xt_g[:], xt_w[:].indirect(l1[:]))
-        nc.vector.tensor_copy(xt_gs[:], xt_s[:].indirect(l1[:]))
-        nc.vector.tensor_copy(xo_g[:], xo_w[:].indirect(l2[:]))
-        nc.vector.tensor_copy(xo_gs[:], xo_s[:].indirect(l2[:]))
-
-        w0_w0 = deal_first("w0_w0", w0_w, U16)
-        w_w0 = deal_first("w_w0", w_w, U32)
-        spread(w0_s, R)
-        spread(w_s, R)
-        w0_s0 = deal_first("w0_s0", w0_s, U8)
-        w_s0 = deal_first("w_s0", w_s, U8)
-
         def product_a(t, w0c, w0s, wc, ws):
             acc = psum.tile([P, J], F32, name="acc_a", bufs=3)
-            nc.tensor.matmul_mx(out=acc[:], lhsT=w0c.bitcast(E2M1), lhsT_scale=w0s, rhs=xo_g[:].bitcast(E4M3),
-                                rhs_scale=xo_gs[:], start=True, stop=False)
             nc.tensor.matmul_mx(out=acc[:], lhsT=wc.bitcast(E4M3), lhsT_scale=ws, rhs=xt_g[:].bitcast(E2M1),
-                                rhs_scale=xt_gs[:], start=False, stop=True)
+                                rhs_scale=xt_gs[:], start=True, stop=False)
+            nc.tensor.matmul_mx(out=acc[:], lhsT=w0c.bitcast(E2M1), lhsT_scale=w0s, rhs=xo_g[:].bitcast(E4M3),
+                                rhs_scale=xo_gs[:], start=False, stop=True)
             a_t = tile("a%d" % t, J, F32)
             if t == 0:
                 nc.scalar.copy(a_t[:], acc[:])
@@ -153,53 +150,39 @@ def tile_list_ownthree_noted_one_ownpage_kernel(
                 nc.vector.tensor_copy(a_t[:], acc[:])
             nc.scalar.activation(boards[t][:].indirect(l3[:]), a_t[:], COPY)
 
-        product_a(0, w0_w0[:], w0_s0[:], w_w0[:], w_s0[:])
+        for t in range(PACK):
+            cols = slice(t * P, (t + 1) * P)
+            product_a(t, w0_wd[:, cols], w0_sd[:, cols], w_wd[:, cols], w_sd[:, cols])
 
-        w0_w1 = deal_rest("w0_w1", w0_w, U16, 8)
-        w_w1 = deal_rest("w_w1", w_w, U32, 4)
-        w0_s1 = deal_rest("w0_s1", w0_s, U8, 16)
-        w_s1 = deal_rest("w_s1", w_s, U8, 16)
-
-        hid = held.tile([P, O, PACK], BF16, name="hid", align_bytes=64)
-
-        def later_a(t):
-            cols = slice((t - 1) * P, t * P)
-            product_a(t, w0_w1[:, cols], w0_s1[:, cols], w_w1[:, cols], w_s1[:, cols])
-
-        later_a(1)
-
-        w2_wd = deal_all("w2_wd", w2_w, U32, 4)
+        w2_wd = deal_all(nc.vector.tensor_copy, "w2_wd", w2_w, U32, 4)
         spread(w2_s, R)
-        w2_sd = deal_all("w2_sd", w2_s, U8, 16)
-
-        def combine(t):
+        w2_sd = deal_all(nc.vector.tensor_copy, "w2_sd", w2_s, U8, 16)
+        seconds = []
+        for t in range(PACK):
             cols = slice(t * P, (t + 1) * P)
             acc = psum.tile([P, J], F32, name="acc_b", bufs=3)
             nc.tensor.matmul_mx(out=acc[:], lhsT=w2_wd[:, cols].bitcast(E5M2), lhsT_scale=w2_sd[:, cols],
                                 rhs=xo_g[:].bitcast(E4M3), rhs_scale=xo_gs[:], start=True, stop=True)
             b_t = tile("b%d" % t, J, F32)
             nc.vector.tensor_copy(b_t[:], acc[:])
-            left = tile("left%d" % t, O, F32)
-            right = tile("right%d" % t, O, F32)
-            third = tile("third%d" % t, O, F32)
-            nc.scalar.activation(left[:], boards[t][:].indirect(l4[:]), COPY, scale=sa_t[:, t : t + 1])
-            nc.scalar.activation(right[:], boards[t][:].indirect(l5[:]), COPY, scale=sb_t[:, t : t + 1])
-            nc.scalar.activation(third[:], b_t[:].indirect(l6[:]), COPY, scale=sd_t[:, t : t + 1])
-            larger = tile("larger%d" % t, O, F32)
-            nc.vector.tensor_tensor(larger[:], left[:], right[:], ALU.max)
-            nc.vector.tensor_tensor(hid[:, :, t], larger[:], third[:], ALU.subtract)
+            seconds.append(b_t)
 
+        hid = held.tile([P, O, PACK], BF16, name="hid", align_bytes=64)
+        picked = tile("picked", 3 * PACK * O, F32, tag="w2_wd")
         for t in range(PACK):
-            combine(t)
-            if t + 2 < PACK:
-                later_a(t + 2)
+            left, right, third = (picked[:, (3 * t + i) * O : (3 * t + i + 1) * O] for i in range(3))
+            nc.scalar.activation(left, boards[t][:].indirect(l4[:]), COPY, scale=sa_t[:, t : t + 1])
+            nc.scalar.activation(right, boards[t][:].indirect(l5[:]), COPY, scale=sb_t[:, t : t + 1])
+            nc.scalar.activation(third, seconds[t][:].indirect(l6[:]), COPY, scale=sd_t[:, t : t + 1])
+            larger = tile("larger%d" % t, O, F32)
+            nc.vector.tensor_tensor(larger[:], left, right, ALU.max)
+            nc.vector.tensor_tensor(hid[:, :, t], larger[:], third, ALU.subtract)
 
         pages = []
         for u in range(N // P):
-            page = tile("page%d" % u, E, F32)
+            page = tile("page%d" % u, E, F32, tag=("w_w", "w2_w")[u])
             nc.vector.memset(page[:], 0.0)
             pages.append(page)
-        spread(wb_s, N)
 
         hid_q = tile("hid_q", O, U32)
         hid_s = tile("hid_s", O, U8)

from contextlib import ExitStack

import concourse.mybir as mybir

T, J, R, Z, C, O, N, E = 1024, 256, 512, 1024, 512, 128, 256, 512
FLOPS = 436207616

F32 = mybir.dt.float32
BF16 = mybir.dt.bfloat16
I32 = mybir.dt.int32
U32 = mybir.dt.uint32
U16 = mybir.dt.uint16
U8 = mybir.dt.uint8
E4M3 = mybir.dt.float8_e4m3fn_x4
E5M2 = mybir.dt.float8_e5m2_x4
E2M1 = mybir.dt.float4_e2m1fn_x4
COPY = mybir.ActivationFunctionType.Copy
ALU = mybir.AluOpType

P = 128
PACK = 4
LINE = 16


def tile_list_ownthree_noted_one_ownpage_kernel(
    tc, xt_words, xt_scales, xo_words, xo_scales, w_words, w_scales, w0_words, w0_scales, w2_words, w2_scales,
    sa, sb, sd, wb_words, wb_scales, offs, offs2, offs3, offs4, offs5, offs6, offs7, out,
):
    nc = tc.nc
    with ExitStack() as ctx:
        held = ctx.enter_context(tc.tile_pool(name="held", bufs=1))
        psum = ctx.enter_context(tc.psum_pool(name="psum", bufs=1))

        def tile(name, cols, dtype, tag=""):
            return held.tile([P, cols], dtype, name=name, tag=tag or name, align_bytes=64)

        def load_list(name, src):
            lst = held.tile(list(src.shape), U16, name=name)
            nc.sync.dma_start(lst[:], src)
            return lst

        def load_words(queue, name, src, cols, dtype):
            words = tile(name, cols, dtype)
            queue.dma_start(words[:].bitcast(I32), src.bitcast(I32))
            return words

        def load_factor(name, src):
            fac = held.tile([P, PACK], F32, name=name)
            nc.sync.dma_start(fac[:], src.rearrange("(p t) o -> p (t o)", t=PACK))
            return fac

        def zeroed(name, cols):
            plane = tile(name, cols, U8)
            nc.vector.memset(plane[:].bitcast(I32), 0)
            return plane

        def load_plane(queue, plane, src):
            for q in range(4):
                queue.dma_start(plane[32 * q : 32 * q + 4, :].bitcast(I32), src[0, 4 * q : 4 * q + 4, :].bitcast(I32))

        def load_halves(queue, plane, src):
            rows = src[0].bitcast(I32).rearrange("(a b r) n -> b r a n", a=2, b=2)
            for b in range(2):
                queue.dma_start(plane[32 * b : 32 * b + 4, :].bitcast(I32).rearrange("r (a n) -> r a n", a=2), rows[b])

        def spread(plane, cols):
            nc.vector.tensor_copy(plane[64:128, 0:cols].bitcast(I32), plane[0:64, cols : 2 * cols].bitcast(I32))

        def deal_all(copy, name, src, dtype, run):
            dealt = tile(name, R, dtype)
            copy(
                dealt[:].rearrange("p (t c i) -> p c t i", t=PACK, i=run),
                src[:, 0:R].rearrange("p (c i t) -> p c t i", i=run, t=PACK),
            )
            return dealt

        flat = lambda words: words[0].rearrange("p n t -> p (n t)")

        w0_s = zeroed("w0_s", 2 * R)
        w_s = zeroed("w_s", 2 * R)
        xt_h = zeroed("xt_h", 2 * T)
        xo_h = zeroed("xo_h", 2 * Z)
        w2_s = zeroed("w2_s", 2 * R)
        wb_s = zeroed("wb_s", N)

        l1 = load_list("l1", offs)
        l2 = load_list("l2", offs2)
        xt_w = load_words(nc.sync, "xt_w", xt_words[0], T, U16)
        load_halves(nc.sync, w0_s, w0_scales)
        load_halves(nc.sync, w_s, w_scales)
        xo_w = load_words(nc.sync, "xo_w", flat(xo_words), Z, U32)
        load_halves(nc.sync, xt_h, xt_scales)
        load_halves(nc.sync, xo_h, xo_scales)
        w0_w = load_words(nc.sync, "w0_w", w0_words[0], R, U16)
        w_w = load_words(nc.sync, "w_w", flat(w_words), R, U32)
        l3 = load_list("l3", offs3)
        w2_w = load_words(nc.sync, "w2_w", flat(w2_words), R, U32)
        l4 = load_list("l4", offs4)
        sa_t = load_factor("sa_t", sa)
        l5 = load_list("l5", offs5)
        sb_t = load_factor("sb_t", sb)
        load_halves(nc.sync, w2_s, w2_scales)
        l6 = load_list("l6", offs6)
        sd_t = load_factor("sd_t", sd)
        wb_w = load_words(nc.sync, "wb_w", wb_words[0], N, U16)
        load_plane(nc.sync, wb_s, wb_scales)
        l7 = load_list("l7", offs7)

        xt_g = tile("xt_g", J, U16)
        xt_gs = tile("xt_gs", J, U8)
        xo_g = tile("xo_g", J, U32)
        xo_gs = tile("xo_gs", J, U8)
        nc.vector.tensor_copy(xt_g[:], xt_w[:].indirect(l1[:]))
        spread(w0_s, R)
        spread(w_s, R)
        w0_sd = deal_all(nc.vector.tensor_copy, "w0_sd", w0_s, U8, 16)
        w_sd = deal_all(nc.vector.tensor_copy, "w_sd", w_s, U8, 16)
        nc.vector.tensor_copy(xo_g[:], xo_w[:].indirect(l2[:]))

        xt_s = tile("xt_s", T, U8)
        xo_s = tile("xo_s", Z, U8)
        for half in range(2):
            for plane, halves, cols in ((xt_s, xt_h, T), (xo_s, xo_h, Z)):
                nc.vector.tensor_copy(
                    plane[64 * half : 64 * half + 64, :].bitcast(I32),
                    halves[0:64, half * cols : (half + 1) * cols].bitcast(I32),
                )
        nc.vector.tensor_copy(xt_gs[:], xt_s[:].indirect(l1[:]))
        nc.vector.tensor_copy(xo_gs[:], xo_s[:].indirect(l2[:]))

        w0_wd = deal_all(nc.scalar.copy, "w0_wd", w0_w, U16, 8)
        w_wd = deal_all(nc.scalar.copy, "w_wd", w_w, U32, 4)

        boards = []
        for t in range(PACK):
            board = tile("board%d" % t, C, F32)
            nc.vector.memset(board[:], 0.0)
            boards.append(board)

        def product_a(t, w0c, w0s, wc, ws):
            acc = psum.tile([P, J], F32, name="acc_a", bufs=3)
            nc.tensor.matmul_mx(out=acc[:], lhsT=wc.bitcast(E4M3), lhsT_scale=ws, rhs=xt_g[:].bitcast(E2M1),
                                rhs_scale=xt_gs[:], start=True, stop=False)
            nc.tensor.matmul_mx(out=acc[:], lhsT=w0c.bitcast(E2M1), lhsT_scale=w0s, rhs=xo_g[:].bitcast(E4M3),
                                rhs_scale=xo_gs[:], start=False, stop=True)
            a_t = tile("a%d" % t, J, F32)
            if t == 0:
                nc.scalar.copy(a_t[:], acc[:])
            else:
                nc.vector.tensor_copy(a_t[:], acc[:])
            nc.scalar.activation(boards[t][:].indirect(l3[:]), a_t[:], COPY)

        for t in range(PACK):
            cols = slice(t * P, (t + 1) * P)
            product_a(t, w0_wd[:, cols], w0_sd[:, cols], w_wd[:, cols], w_sd[:, cols])

        w2_wd = deal_all(nc.vector.tensor_copy, "w2_wd", w2_w, U32, 4)
        spread(w2_s, R)
        w2_sd = deal_all(nc.vector.tensor_copy, "w2_sd", w2_s, U8, 16)
        seconds = []
        for t in range(PACK):
            cols = slice(t * P, (t + 1) * P)
            acc = psum.tile([P, J], F32, name="acc_b", bufs=3)
            nc.tensor.matmul_mx(out=acc[:], lhsT=w2_wd[:, cols].bitcast(E5M2), lhsT_scale=w2_sd[:, cols],
                                rhs=xo_g[:].bitcast(E4M3), rhs_scale=xo_gs[:], start=True, stop=True)
            b_t = tile("b%d" % t, J, F32)
            nc.vector.tensor_copy(b_t[:], acc[:])
            seconds.append(b_t)

        hid = held.tile([P, O, PACK], BF16, name="hid", align_bytes=64)
        picked = tile("picked", 3 * PACK * O, F32, tag="w2_wd")
        for t in range(PACK):
            left, right, third = (picked[:, (3 * t + i) * O : (3 * t + i + 1) * O] for i in range(3))
            nc.scalar.activation(left, boards[t][:].indirect(l4[:]), COPY, scale=sa_t[:, t : t + 1])
            nc.scalar.activation(right, boards[t][:].indirect(l5[:]), COPY, scale=sb_t[:, t : t + 1])
            nc.scalar.activation(third, seconds[t][:].indirect(l6[:]), COPY, scale=sd_t[:, t : t + 1])
            larger = tile("larger%d" % t, O, F32)
            nc.vector.tensor_tensor(larger[:], left, right, ALU.max)
            nc.vector.tensor_tensor(hid[:, :, t], larger[:], third, ALU.subtract)

        pages = []
        for u in range(N // P):
            page = tile("page%d" % u, E, F32, tag=("w_w", "w2_w")[u])
            nc.vector.memset(page[:], 0.0)
            pages.append(page)

        hid_q = tile("hid_q", O, U32)
        hid_s = tile("hid_s", O, U8)
        nc.vector.quantize_mx(out=hid_q[:].bitcast(E5M2), scales=hid_s[:], in_=hid[:].rearrange("p o t -> p (o t)"))

        for u in range(N // P):
            cols = slice(u * P, (u + 1) * P)
            acc = psum.tile([P, O], F32, name="acc_p", bufs=2)
            nc.tensor.matmul_mx(out=acc[:], lhsT=wb_w[:, cols].bitcast(E2M1), lhsT_scale=wb_s[:, cols],
                                rhs=hid_q[:].bitcast(E5M2), rhs_scale=hid_s[:], start=True, stop=True)
            p_u = tile("p%d" % u, O, F32)
            nc.vector.tensor_copy(p_u[:], acc[:])
            nc.scalar.activation(pages[u][:].indirect(l7[:]), p_u[:], COPY)
            nc.sync.dma_start(out[u * P : (u + 1) * P, :], pages[u][:])
